import numpy as np
import ml_dtypes


def mxq(x, axis, fmt="e4m3"):
    dtype, down = {"e4m3": (ml_dtypes.float8_e4m3fn, 7), "e5m2": (ml_dtypes.float8_e5m2, 14)}[fmt]
    v = np.moveaxis(np.asarray(x, np.float32).astype(ml_dtypes.bfloat16).astype(np.float64), axis, -1)
    blocks = v.reshape(v.shape[:-1] + (-1, 32))
    amax = np.abs(blocks).max(-1, keepdims=True)
    byte = np.maximum(np.where(amax > 0, np.frexp(amax)[1] - 1 + 127, 0) - down, 1)
    scale = np.exp2(byte - 127.0)
    codes = (blocks / scale).astype(np.float32).astype(dtype).astype(np.float64)
    return np.moveaxis((codes * scale).reshape(v.shape), -1, axis)


WIDE = False


def mx_kscale(k):
    if not WIDE:
        return np.ones(k)
    levels = np.array([10, -10, 5, -5, 0])
    if k % 512:
        return np.exp2(np.random.permutation(np.resize(levels, k // 32))).repeat(32)
    a = np.empty((k // 512, 16))
    for p in range(k // 512):
        a[p, :8] = np.random.permutation(np.resize(levels, 8))
        for g in range(8):
            far = levels[np.abs(levels - a[p, g]) >= 10]
            a[p, g + 8] = far[np.random.randint(len(far))]
    return np.exp2(a.ravel()).repeat(32)


def f64(x):
    return np.asarray(x).astype(np.float64)


def striped(idx):
    return np.tile(idx.reshape(-1, 16).T, (8, 1)).astype(np.uint16)


def unstriped(offs):
    return offs[:16].T.reshape(-1).astype(np.int64)


def striped8(idx):
    return np.concatenate([x.reshape(-1, 16).T for x in idx]).astype(np.uint16)


def runs(offs, k):
    lists = np.stack([offs[16 * r : 16 * r + 16].T.reshape(-1) for r in range(8)]).astype(np.int64)
    return lists[np.arange(k) % 512 // 64]


def pack_weight(w):
    k, n = w.shape
    w = f64(np.asarray(w, np.float32).astype(ml_dtypes.bfloat16)).reshape(k // 32, 32, n)
    amax = np.abs(w).max(1)
    byte = np.clip(np.where(amax > 0, np.frexp(amax)[1] - 1 + 127 - 7, 1), 1, 254)
    scaled = (w * np.exp2(127.0 - byte)[:, None, :]).reshape(k, n).astype(np.float32)
    words = np.ascontiguousarray(scaled.reshape(k // 512, 128, 4, n).transpose(0, 1, 3, 2)).astype(ml_dtypes.float8_e4m3fn).view(np.uint8)
    return words, np.ascontiguousarray(byte.astype(np.uint8).reshape(k // 512, 16, n))


def unpack_weight(words, scales):
    g, p, n, _ = words.shape
    vals = np.ascontiguousarray(words).view(ml_dtypes.float8_e4m3fn).astype(np.float64) * np.repeat(np.exp2(scales.astype(np.float64) - 127.0), 8, axis=1)[..., None]
    return vals.transpose(0, 1, 3, 2).reshape(g * 512, n)


K, T, S, H, G, W = 512, 2048, 256, 512, 2048, 128


def setup_inputs():
    n = np.random.standard_normal
    s = mx_kscale(K)[:, None]
    packed_xT = pack_weight(n((K, T)) * s)
    packed_dT = pack_weight(n((K, G)) / s)
    perm = np.random.permutation(S)
    return {
        "x_words": packed_xT[0],
        "x_scales": packed_xT[1],
        "w1": (n((K, H)) / np.sqrt(K) / s).astype(np.float32),
        "gs": (np.random.uniform(0.5, 1.5, (K, 1)) * s).astype(np.float32),
        "d_words": packed_dT[0],
        "d_scales": packed_dT[1],
        "offs": striped8(np.random.randint(0, T, (8, S))),
        "ka": striped8(np.random.randint(0, G, (8, H))),
        "kb": striped8(np.random.randint(0, G, (8, H))),
        "n1": striped(perm[:W]),
        "n2": striped(perm[W:]),
    }


def reference(x_words, x_scales, w1, gs, d_words, d_scales, offs, ka, kb, n1, n2):
    d_ka = unpack_weight(d_words, d_scales)[np.arange(K)[:, None], runs(ka, K)]
    xq = unpack_weight(x_words, x_scales)[np.arange(K)[:, None], runs(offs, K)]
    y = mxq(f64(w1), 0, "e4m3").T @ xq
    z = f64(gs) * y
    zq = mxq(z, 0, "e4m3")
    d_kb = unpack_weight(d_words, d_scales)[np.arange(K)[:, None], runs(kb, K)]
    h = 0.0625 * (d_ka.T @ zq + d_kb.T @ zq)
    pa = h[:, unstriped(n1)]
    pb = h[:, unstriped(n2)]
    rb = np.maximum(pa, pb)
    ra = pa / (np.abs(pb) + 0.5)
    ds = np.zeros((H, S))
    ds[:, unstriped(n1)] = ra
    out = ds.copy()
    out[:, unstriped(n2)] = rb
    return out

@@ -1,0 +1,173 @@
+from contextlib import ExitStack
+
+import concourse.mybir as mybir
+
+K, T, S, H, G, W = 512, 2048, 256, 512, 2048, 128
+FLOPS = 2 * K * H * S * 3
+
+F32 = mybir.dt.float32
+BF16 = mybir.dt.bfloat16
+I32 = mybir.dt.int32
+U32 = mybir.dt.uint32
+U16 = mybir.dt.uint16
+U8 = mybir.dt.uint8
+FP8X4 = mybir.dt.float8_e4m3fn_x4
+ALU = mybir.AluOpType
+COPY = mybir.ActivationFunctionType.Copy
+
+P = 128
+PACK = 4
+HALF = 256
+
+
+def tile_picked_hdaqiratio_none_p_kernel(tc, x_words, x_scales, w1, gs, d_words, d_scales, offs, ka, kb, n1, n2, out):
+    nc = tc.nc
+    with ExitStack() as ctx:
+        keep = ctx.enter_context(tc.tile_pool(name="keep", bufs=1))
+        psum = ctx.enter_context(tc.psum_pool(name="psum", bufs=1))
+
+        def load_list(src, name):
+            t = keep.tile(list(src.shape), U16, name=name)
+            nc.sync.dma_start(t[:], src)
+            return t
+
+        def scale_window(src, name, tag):
+            t = keep.tile([P, T], U8, name=name, tag=tag, align_bytes=64)
+            nc.vector.memset(t[:].bitcast(I32), 0)
+            nc.scalar.dma_start(t[:].bitcast(I32)[0:P:8, :], src[0].bitcast(I32))
+            return t
+
+        def word_window(src, name, tag):
+            t = keep.tile([P, T], I32, name=name, tag=tag, align_bytes=64)
+            nc.sync.dma_start(t[:], src[0].rearrange("p n t -> p (n t)").bitcast(I32))
+            return t
+
+        def place_rows(plane, picked):
+            for s in range(4):
+                nc.scalar.dma_start(plane[:].bitcast(I32)[s:P:32, :], picked[:].bitcast(I32)[8 * s:P:32, :])
+
+        xs_win = scale_window(x_scales, "xs_win", "xs_then_dw")
+        ds_win = scale_window(d_scales, "ds_win", "ds_win")
+        offs_t = load_list(offs, "offs_t")
+        ka_t = load_list(ka, "ka_t")
+        kb_t = load_list(kb, "kb_t")
+        w_raw = keep.tile([P, PACK, H], F32, name="w_raw")
+        nc.sync.dma_start(w_raw[:], w1.rearrange("(p j) c -> p j c", j=PACK))
+        n1_t = load_list(n1, "n1_t")
+        n2_t = load_list(n2, "n2_t")
+        xw_win = word_window(x_words, "xw_win", "xw_win")
+        gs_t = keep.tile([P, PACK], F32, name="gs_t")
+        nc.gpsimd.dma_start(gs_t[:], gs.rearrange("(p t) o -> p (t o)", t=PACK))
+
+        x_plane = keep.tile([P, S], U8, name="x_plane", align_bytes=64)
+        d_plane = keep.tile([P, 2 * H], U8, name="d_plane", align_bytes=64)
+        nc.vector.memset(x_plane[:].bitcast(I32), 0)
+        nc.vector.memset(d_plane[:].bitcast(I32), 0)
+
+        xs_pick = keep.tile([P, S], U8, name="xs_pick", align_bytes=64)
+        nc.vector.tensor_copy(xs_pick[:], xs_win[:].indirect(offs_t[:]))
+        place_rows(x_plane, xs_pick)
+        dw_win = word_window(d_words, "dw_win", "xs_then_dw")
+
+        ds_pick = keep.tile([P, 2 * H], U8, name="ds_pick", align_bytes=64)
+        nc.vector.tensor_copy(ds_pick[:, 0:H], ds_win[:].indirect(ka_t[:]))
+        nc.vector.tensor_copy(ds_pick[:, H:2 * H], ds_win[:].indirect(kb_t[:]))
+
+        w_bf = keep.tile([P, PACK, P, PACK], BF16, name="w_bf", align_bytes=64)
+        w_src = w_raw[:].rearrange("p j (m t) -> p m t j", t=PACK)
+        w_dst = w_bf[:].rearrange("p t m j -> p m t j")
+        for c in range(4):
+            nc.scalar.activation(w_dst[:, 32 * c:32 * c + 32], w_src[:, 32 * c:32 * c + 32], COPY)
+        place_rows(d_plane, ds_pick)
+
+        w_codes = keep.tile([P, H], U32, name="w_codes", align_bytes=64)
+        w_plane = keep.tile([P, H], U8, name="w_plane", align_bytes=64)
+        nc.vector.quantize_mx(out=w_codes[:].bitcast(FP8X4), scales=w_plane[:], in_=w_bf[:].rearrange("p t m j -> p (t m j)"))
+
+        x_codes = keep.tile([P, S], U32, name="x_codes", align_bytes=64)
+        nc.vector.tensor_copy(x_codes[:], xw_win[:].bitcast(U32).indirect(offs_t[:]))
+
+        z_bf = keep.tile([P, S, PACK], BF16, name="z_bf", align_bytes=64)
+        z_codes = keep.tile([P, S], U32, name="z_codes", align_bytes=64)
+        z_plane = keep.tile([P, S], U8, name="z_plane", align_bytes=64)
+        gs_b = gs_t[:].unsqueeze(1).broadcast_to([P, P, PACK])
+        for u in range(2):
+            cols = slice(P * u, P * u + P)
+            y = psum.tile([P, PACK, P], F32, name="y%d" % u)
+            for t in range(PACK):
+                nc.tensor.matmul_mx(
+                    out=y[:, t, :],
+                    lhsT=w_codes[:, P * t:P * t + P].bitcast(FP8X4),
+                    lhsT_scale=w_plane[:, P * t:P * t + P],
+                    rhs=x_codes[:, cols].bitcast(FP8X4),
+                    rhs_scale=x_plane[:, cols],
+                    start=True,
+                    stop=True,
+                )
+            nc.vector.tensor_tensor(z_bf[:, cols, :], y[:].rearrange("p t n -> p n t"), gs_b, ALU.mult)
+        for u in range(2):
+            cols = slice(P * u, P * u + P)
+            nc.vector.quantize_mx(out=z_codes[:, cols].bitcast(FP8X4), scales=z_plane[:, cols], in_=z_bf[:, cols, :].rearrange("p n t -> p (n t)"))
+
+        d_codes = []
+        for u in range(2):
+            pair = []
+            for lst, name in ((ka_t, "a"), (kb_t, "b")):
+                c = keep.tile([P, HALF], U32, name="d%s_codes%d" % (name, u), align_bytes=64)
+                nc.vector.tensor_copy(c[:], dw_win[:].bitcast(U32).indirect(lst[:, 16 * u:16 * u + 16]))
+                pair.append(c)
+            d_codes.append(pair)
+
+        pa, pb, o = [], [], []
+
+        def fetch(i):
+            acc = psum.tile([P, S], F32, name="acc%d" % i)
+            for e in range(2):
+                c0 = P * (i % 2)
+                s0 = H * e + P * i
+                nc.tensor.matmul_mx(
+                    out=acc[:],
+                    lhsT=d_codes[i // 2][e][:, c0:c0 + P].bitcast(FP8X4),
+                    lhsT_scale=d_plane[:, s0:s0 + P],
+                    rhs=z_codes[:].bitcast(FP8X4),
+                    rhs_scale=z_plane[:],
+                    start=(e == 0),
+                    stop=(e == 1),
+                )
+            h = keep.tile([P, S], F32, name="h%d" % i)
+            if i == 0:
+                nc.scalar.activation(h[:], acc[:], COPY, scale=0.0625)
+            else:
+                nc.vector.tensor_scalar(h[:], acc[:], 0.0625, None, ALU.mult)
+            b = keep.tile([P, W], F32, name="pb%d" % i)
+            a = keep.tile([P, W], F32, name="pa%d" % i)
+            nc.scalar.activation(b[:], h[:].indirect(n2_t[:]), COPY)
+            nc.scalar.activation(a[:], h[:].indirect(n1_t[:]), COPY)
+            pa.append(a)
+            pb.append(b)
+
+        def finish(i):
+            a, b = pa[i], pb[i]
+            flip = keep.tile([P, W], F32, name="flip%d" % i)
+            den = keep.tile([P, W], F32, name="den%d" % i)
+            inv = keep.tile([P, W], F32, name="inv%d" % i)
+            ra = keep.tile([P, W], F32, name="ra%d" % i)
+            rb = keep.tile([P, W], F32, name="rb%d" % i)
+            res = keep.tile([P, S], F32, name="res%d" % i)
+            nc.vector.tensor_scalar(flip[:], b[:], -1.0, 0.5, ALU.mult, ALU.add)
+            nc.vector.tensor_tensor(rb[:], a[:], b[:], ALU.max)
+            nc.vector.scalar_tensor_tensor(den[:], b[:], 0.5, flip[:], ALU.add, ALU.max)
+            nc.vector.reciprocal(inv[:], den[:])
+            nc.vector.tensor_tensor(ra[:], a[:], inv[:], ALU.mult)
+            nc.scalar.activation(res[:].indirect(n2_t[:]), rb[:], COPY)
+            nc.scalar.activation(res[:].indirect(n1_t[:]), ra[:], COPY)
+            nc.sync.dma_start(out[P * i:P * i + P, :], res[:])
+
+        fetch(0)
+        fetch(1)
+        finish(0)
+        fetch(2)
+        finish(1)
+        fetch(3)
+        finish(2)
+        finish(3)

@@ -34,7 +34,7 @@ def tile_picked_hdaqiratio_none_p_kernel(tc, x_words, x_scales, w1, gs, d_words,
         def scale_window(src, name, tag):
             t = keep.tile([P, T], U8, name=name, tag=tag, align_bytes=64)
             nc.vector.memset(t[:].bitcast(I32), 0)
-            nc.scalar.dma_start(t[:].bitcast(I32)[0:P:8, :], src[0].bitcast(I32))
+            nc.sync.dma_start(t[:].bitcast(I32)[0:P:8, :], src[0].bitcast(I32))
             return t
 
         def word_window(src, name, tag):
@@ -42,50 +42,62 @@ def tile_picked_hdaqiratio_none_p_kernel(tc, x_words, x_scales, w1, gs, d_words,
             nc.sync.dma_start(t[:], src[0].rearrange("p n t -> p (n t)").bitcast(I32))
             return t
 
-        def place_rows(plane, picked):
+        def place_rows(queue, plane, picked):
             for s in range(4):
-                nc.scalar.dma_start(plane[:].bitcast(I32)[s:P:32, :], picked[:].bitcast(I32)[8 * s:P:32, :])
+                queue.dma_start(plane.bitcast(I32)[s:P:32, :], picked.bitcast(I32)[8 * s:P:32, :])
 
-        xs_win = scale_window(x_scales, "xs_win", "xs_then_dw")
-        ds_win = scale_window(d_scales, "ds_win", "ds_win")
+        w_rows = w1.rearrange("(p j) c -> p j c", j=PACK)
         offs_t = load_list(offs, "offs_t")
+        w_lo = keep.tile([P, 2, H], F32, name="w_lo")
+        nc.sync.dma_start(w_lo[:], w_rows[:, 0:2, :])
         ka_t = load_list(ka, "ka_t")
         kb_t = load_list(kb, "kb_t")
-        w_raw = keep.tile([P, PACK, H], F32, name="w_raw")
-        nc.sync.dma_start(w_raw[:], w1.rearrange("(p j) c -> p j c", j=PACK))
-        n1_t = load_list(n1, "n1_t")
-        n2_t = load_list(n2, "n2_t")
-        xw_win = word_window(x_words, "xw_win", "xw_win")
+        xs_win = scale_window(x_scales, "xs_win", "xs_then_dw")
+        ds_win = scale_window(d_scales, "ds_win", "ds_win")
+        w_hi = keep.tile([P, 2, H], F32, name="w_hi")
+        nc.sync.dma_start(w_hi[:], w_rows[:, 2:4, :])
         gs_t = keep.tile([P, PACK], F32, name="gs_t")
-        nc.gpsimd.dma_start(gs_t[:], gs.rearrange("(p t) o -> p (t o)", t=PACK))
+        nc.sync.dma_start(gs_t[:], gs.rearrange("(p t) o -> p (t o)", t=PACK))
+        xw_win = word_window(x_words, "xw_win", "xw_then_late")
 
-        x_plane = keep.tile([P, S], U8, name="x_plane", align_bytes=64)
-        d_plane = keep.tile([P, 2 * H], U8, name="d_plane", align_bytes=64)
-        nc.vector.memset(x_plane[:].bitcast(I32), 0)
-        nc.vector.memset(d_plane[:].bitcast(I32), 0)
+        early_plane = keep.tile([P, 3 * HALF], U8, name="early_plane", align_bytes=64)
+        late_plane = keep.tile([P, 2 * HALF], U8, name="late_plane", align_bytes=64)
+        for plane in (early_plane, late_plane):
+            nc.vector.memset(plane[:].bitcast(I32), 0)
+        x_plane = early_plane[:, 0:S]
+        d_planes = [early_plane[:, S:S + 2 * HALF], late_plane[:]]
 
-        xs_pick = keep.tile([P, S], U8, name="xs_pick", align_bytes=64)
-        nc.vector.tensor_copy(xs_pick[:], xs_win[:].indirect(offs_t[:]))
-        place_rows(x_plane, xs_pick)
+        def pick_d_scales(picked, u):
+            for e, lst in enumerate((ka_t, kb_t)):
+                nc.vector.tensor_copy(picked[:, HALF * e:HALF * e + HALF], ds_win[:].indirect(lst[:, 16 * u:16 * u + 16]))
+
+        early_pick = keep.tile([P, 3 * HALF], U8, name="early_pick", align_bytes=64)
+        nc.vector.tensor_copy(early_pick[:, 0:S], xs_win[:].indirect(offs_t[:]))
+        pick_d_scales(early_pick[:, S:S + 2 * HALF], 0)
+        place_rows(nc.sync, early_plane[:], early_pick[:])
         dw_win = word_window(d_words, "dw_win", "xs_then_dw")
-
-        ds_pick = keep.tile([P, 2 * H], U8, name="ds_pick", align_bytes=64)
-        nc.vector.tensor_copy(ds_pick[:, 0:H], ds_win[:].indirect(ka_t[:]))
-        nc.vector.tensor_copy(ds_pick[:, H:2 * H], ds_win[:].indirect(kb_t[:]))
-
-        w_bf = keep.tile([P, PACK, P, PACK], BF16, name="w_bf", align_bytes=64)
-        w_src = w_raw[:].rearrange("p j (m t) -> p m t j", t=PACK)
-        w_dst = w_bf[:].rearrange("p t m j -> p m t j")
-        for c in range(4):
-            nc.scalar.activation(w_dst[:, 32 * c:32 * c + 32], w_src[:, 32 * c:32 * c + 32], COPY)
-        place_rows(d_plane, ds_pick)
+        n2_t = load_list(n2, "n2_t")
+        n1_t = load_list(n1, "n1_t")
 
         w_codes = keep.tile([P, H], U32, name="w_codes", align_bytes=64)
         w_plane = keep.tile([P, H], U8, name="w_plane", align_bytes=64)
-        nc.vector.quantize_mx(out=w_codes[:].bitcast(FP8X4), scales=w_plane[:], in_=w_bf[:].rearrange("p t m j -> p (t m j)"))
+        lo_src = w_lo[:].rearrange("p j (m t) -> p m j t", t=PACK)
+        hi_src = w_hi[:].rearrange("p j (m t) -> p m j t", t=PACK)
+        w_bf = [keep.tile([P, 2, P, PACK], BF16, name="w_bf%d" % u, align_bytes=64) for u in range(2)]
+        w_dst = [b[:].rearrange("p t m j -> p m j t") for b in w_bf]
+        for u in range(2):
+            nc.scalar.activation(w_dst[u][:, :, 0:2, :], lo_src[:, :, :, 2 * u:2 * u + 2], COPY)
+        for u in range(2):
+            nc.vector.tensor_copy(w_dst[u][:, :, 2:4, :], hi_src[:, :, :, 2 * u:2 * u + 2])
+        for u in range(2):
+            cols = slice(HALF * u, HALF * u + HALF)
+            nc.vector.quantize_mx(out=w_codes[:, cols].bitcast(FP8X4), scales=w_plane[:, cols], in_=w_bf[u][:].rearrange("p t m j -> p (t m j)"))
 
         x_codes = keep.tile([P, S], U32, name="x_codes", align_bytes=64)
         nc.vector.tensor_copy(x_codes[:], xw_win[:].bitcast(U32).indirect(offs_t[:]))
+        late_pick = keep.tile([P, 2 * HALF], U8, name="late_pick", tag="xw_then_late", align_bytes=64)
+        pick_d_scales(late_pick[:], 1)
+        place_rows(nc.scalar, late_plane[:], late_pick[:])
 
         z_bf = keep.tile([P, S, PACK], BF16, name="z_bf", align_bytes=64)
         z_codes = keep.tile([P, S], U32, name="z_codes", align_bytes=64)
@@ -124,11 +136,10 @@ def tile_picked_hdaqiratio_none_p_kernel(tc, x_words, x_scales, w1, gs, d_words,
             acc = psum.tile([P, S], F32, name="acc%d" % i)
             for e in range(2):
                 c0 = P * (i % 2)
-                s0 = H * e + P * i
                 nc.tensor.matmul_mx(
                     out=acc[:],
                     lhsT=d_codes[i // 2][e][:, c0:c0 + P].bitcast(FP8X4),
-                    lhsT_scale=d_plane[:, s0:s0 + P],
+                    lhsT_scale=d_planes[i // 2][:, HALF * e + c0:HALF * e + c0 + P],
                     rhs=z_codes[:].bitcast(FP8X4),
                     rhs_scale=z_plane[:],
                     start=(e == 0),
@@ -163,11 +174,7 @@ def tile_picked_hdaqiratio_none_p_kernel(tc, x_words, x_scales, w1, gs, d_words,
             nc.scalar.activation(res[:].indirect(n1_t[:]), ra[:], COPY)
             nc.sync.dma_start(out[P * i:P * i + P, :], res[:])
 
-        fetch(0)
-        fetch(1)
-        finish(0)
-        fetch(2)
-        finish(1)
-        fetch(3)
-        finish(2)
-        finish(3)
+        for i in range(4):
+            fetch(i)
+        for i in range(4):
+            finish(i)

@@ -47,18 +47,17 @@ def tile_picked_hdaqiratio_none_p_kernel(tc, x_words, x_scales, w1, gs, d_words,
                 queue.dma_start(plane.bitcast(I32)[s:P:32, :], picked.bitcast(I32)[8 * s:P:32, :])
 
         w_rows = w1.rearrange("(p j) c -> p j c", j=PACK)
+        w_raw = keep.tile([P, PACK, H], F32, name="w_raw")
+        nc.sync.dma_start(w_raw[:, 0:2, :], w_rows[:, 0:2, :])
         offs_t = load_list(offs, "offs_t")
-        w_lo = keep.tile([P, 2, H], F32, name="w_lo")
-        nc.sync.dma_start(w_lo[:], w_rows[:, 0:2, :])
         ka_t = load_list(ka, "ka_t")
         kb_t = load_list(kb, "kb_t")
         xs_win = scale_window(x_scales, "xs_win", "xs_then_dw")
         ds_win = scale_window(d_scales, "ds_win", "ds_win")
-        w_hi = keep.tile([P, 2, H], F32, name="w_hi")
-        nc.sync.dma_start(w_hi[:], w_rows[:, 2:4, :])
+        nc.sync.dma_start(w_raw[:, 2:4, :], w_rows[:, 2:4, :])
+        xw_win = word_window(x_words, "xw_win", "xw_then_late")
         gs_t = keep.tile([P, PACK], F32, name="gs_t")
         nc.sync.dma_start(gs_t[:], gs.rearrange("(p t) o -> p (t o)", t=PACK))
-        xw_win = word_window(x_words, "xw_win", "xw_then_late")
 
         early_plane = keep.tile([P, 3 * HALF], U8, name="early_plane", align_bytes=64)
         late_plane = keep.tile([P, 2 * HALF], U8, name="late_plane", align_bytes=64)
@@ -81,14 +80,12 @@ def tile_picked_hdaqiratio_none_p_kernel(tc, x_words, x_scales, w1, gs, d_words,
 
         w_codes = keep.tile([P, H], U32, name="w_codes", align_bytes=64)
         w_plane = keep.tile([P, H], U8, name="w_plane", align_bytes=64)
-        lo_src = w_lo[:].rearrange("p j (m t) -> p m j t", t=PACK)
-        hi_src = w_hi[:].rearrange("p j (m t) -> p m j t", t=PACK)
+        w_src = w_raw[:].rearrange("p j (m t) -> p m j t", t=PACK)
         w_bf = [keep.tile([P, 2, P, PACK], BF16, name="w_bf%d" % u, align_bytes=64) for u in range(2)]
         w_dst = [b[:].rearrange("p t m j -> p m j t") for b in w_bf]
-        for u in range(2):
-            nc.scalar.activation(w_dst[u][:, :, 0:2, :], lo_src[:, :, :, 2 * u:2 * u + 2], COPY)
-        for u in range(2):
-            nc.vector.tensor_copy(w_dst[u][:, :, 2:4, :], hi_src[:, :, :, 2 * u:2 * u + 2])
+        nc.scalar.activation(w_dst[0][:, :, 0:2, :], w_src[:, :, 0:2, 0:2], COPY)
+        nc.vector.tensor_copy(w_dst[0][:, :, 2:4, :], w_src[:, :, 2:4, 0:2])
+        nc.scalar.activation(w_dst[1], w_src[:, :, :, 2:4], COPY)
         for u in range(2):
             cols = slice(HALF * u, HALF * u + HALF)
             nc.vector.quantize_mx(out=w_codes[:, cols].bitcast(FP8X4), scales=w_plane[:, cols], in_=w_bf[u][:].rearrange("p t m j -> p (t m j)"))

from contextlib import ExitStack

import concourse.mybir as mybir

K, T, S, H, G, W = 512, 2048, 256, 512, 2048, 128
FLOPS = 2 * K * H * S * 3

F32 = mybir.dt.float32
BF16 = mybir.dt.bfloat16
I32 = mybir.dt.int32
U32 = mybir.dt.uint32
U16 = mybir.dt.uint16
U8 = mybir.dt.uint8
FP8X4 = mybir.dt.float8_e4m3fn_x4
ALU = mybir.AluOpType
COPY = mybir.ActivationFunctionType.Copy

P = 128
PACK = 4
HALF = 256


def tile_picked_hdaqiratio_none_p_kernel(tc, x_words, x_scales, w1, gs, d_words, d_scales, offs, ka, kb, n1, n2, out):
    nc = tc.nc
    with ExitStack() as ctx:
        keep = ctx.enter_context(tc.tile_pool(name="keep", bufs=1))
        psum = ctx.enter_context(tc.psum_pool(name="psum", bufs=1))

        def load_list(src, name):
            t = keep.tile(list(src.shape), U16, name=name)
            nc.sync.dma_start(t[:], src)
            return t

        def scale_window(src, name, tag):
            t = keep.tile([P, T], U8, name=name, tag=tag, align_bytes=64)
            nc.vector.memset(t[:].bitcast(I32), 0)
            nc.sync.dma_start(t[:].bitcast(I32)[0:P:8, :], src[0].bitcast(I32))
            return t

        def word_window(src, name, tag):
            t = keep.tile([P, T], I32, name=name, tag=tag, align_bytes=64)
            nc.sync.dma_start(t[:], src[0].rearrange("p n t -> p (n t)").bitcast(I32))
            return t

        def place_rows(queue, plane, picked):
            for s in range(4):
                queue.dma_start(plane.bitcast(I32)[s:P:32, :], picked.bitcast(I32)[8 * s:P:32, :])

        w_rows = w1.rearrange("(p j) c -> p j c", j=PACK)
        w_raw = keep.tile([P, PACK, H], F32, name="w_raw")
        nc.sync.dma_start(w_raw[:, 0:2, :], w_rows[:, 0:2, :])
        offs_t = load_list(offs, "offs_t")
        ka_t = load_list(ka, "ka_t")
        kb_t = load_list(kb, "kb_t")
        xs_win = scale_window(x_scales, "xs_win", "xs_then_dw")
        ds_win = scale_window(d_scales, "ds_win", "ds_win")
        nc.sync.dma_start(w_raw[:, 2:4, :], w_rows[:, 2:4, :])
        xw_win = word_window(x_words, "xw_win", "xw_then_late")
        gs_t = keep.tile([P, PACK], F32, name="gs_t")
        nc.sync.dma_start(gs_t[:], gs.rearrange("(p t) o -> p (t o)", t=PACK))

        early_plane = keep.tile([P, 3 * HALF], U8, name="early_plane", align_bytes=64)
        late_plane = keep.tile([P, 2 * HALF], U8, name="late_plane", align_bytes=64)
        for plane in (early_plane, late_plane):
            nc.vector.memset(plane[:].bitcast(I32), 0)
        x_plane = early_plane[:, 0:S]
        d_planes = [early_plane[:, S:S + 2 * HALF], late_plane[:]]

        def pick_d_scales(picked, u):
            for e, lst in enumerate((ka_t, kb_t)):
                nc.vector.tensor_copy(picked[:, HALF * e:HALF * e + HALF], ds_win[:].indirect(lst[:, 16 * u:16 * u + 16]))

        early_pick = keep.tile([P, 3 * HALF], U8, name="early_pick", align_bytes=64)
        nc.vector.tensor_copy(early_pick[:, 0:S], xs_win[:].indirect(offs_t[:]))
        pick_d_scales(early_pick[:, S:S + 2 * HALF], 0)
        place_rows(nc.sync, early_plane[:], early_pick[:])
        dw_win = word_window(d_words, "dw_win", "xs_then_dw")
        n2_t = load_list(n2, "n2_t")
        n1_t = load_list(n1, "n1_t")

        w_codes = keep.tile([P, H], U32, name="w_codes", align_bytes=64)
        w_plane = keep.tile([P, H], U8, name="w_plane", align_bytes=64)
        w_src = w_raw[:].rearrange("p j (m t) -> p m j t", t=PACK)
        w_bf = [keep.tile([P, 2, P, PACK], BF16, name="w_bf%d" % u, align_bytes=64) for u in range(2)]
        w_dst = [b[:].rearrange("p t m j -> p m j t") for b in w_bf]
        nc.scalar.activation(w_dst[0][:, :, 0:2, :], w_src[:, :, 0:2, 0:2], COPY)
        nc.vector.tensor_copy(w_dst[0][:, :, 2:4, :], w_src[:, :, 2:4, 0:2])
        nc.scalar.activation(w_dst[1], w_src[:, :, :, 2:4], COPY)
        for u in range(2):
            cols = slice(HALF * u, HALF * u + HALF)
            nc.vector.quantize_mx(out=w_codes[:, cols].bitcast(FP8X4), scales=w_plane[:, cols], in_=w_bf[u][:].rearrange("p t m j -> p (t m j)"))

        x_codes = keep.tile([P, S], U32, name="x_codes", align_bytes=64)
        nc.vector.tensor_copy(x_codes[:], xw_win[:].bitcast(U32).indirect(offs_t[:]))
        late_pick = keep.tile([P, 2 * HALF], U8, name="late_pick", tag="xw_then_late", align_bytes=64)
        pick_d_scales(late_pick[:], 1)
        place_rows(nc.scalar, late_plane[:], late_pick[:])

        z_bf = keep.tile([P, S, PACK], BF16, name="z_bf", align_bytes=64)
        z_codes = keep.tile([P, S], U32, name="z_codes", align_bytes=64)
        z_plane = keep.tile([P, S], U8, name="z_plane", align_bytes=64)
        gs_b = gs_t[:].unsqueeze(1).broadcast_to([P, P, PACK])
        for u in range(2):
            cols = slice(P * u, P * u + P)
            y = psum.tile([P, PACK, P], F32, name="y%d" % u)
            for t in range(PACK):
                nc.tensor.matmul_mx(
                    out=y[:, t, :],
                    lhsT=w_codes[:, P * t:P * t + P].bitcast(FP8X4),
                    lhsT_scale=w_plane[:, P * t:P * t + P],
                    rhs=x_codes[:, cols].bitcast(FP8X4),
                    rhs_scale=x_plane[:, cols],
                    start=True,
                    stop=True,
                )
            nc.vector.tensor_tensor(z_bf[:, cols, :], y[:].rearrange("p t n -> p n t"), gs_b, ALU.mult)
        for u in range(2):
            cols = slice(P * u, P * u + P)
            nc.vector.quantize_mx(out=z_codes[:, cols].bitcast(FP8X4), scales=z_plane[:, cols], in_=z_bf[:, cols, :].rearrange("p n t -> p (n t)"))

        d_codes = []
        for u in range(2):
            pair = []
            for lst, name in ((ka_t, "a"), (kb_t, "b")):
                c = keep.tile([P, HALF], U32, name="d%s_codes%d" % (name, u), align_bytes=64)
                nc.vector.tensor_copy(c[:], dw_win[:].bitcast(U32).indirect(lst[:, 16 * u:16 * u + 16]))
                pair.append(c)
            d_codes.append(pair)

        pa, pb, o = [], [], []

        def fetch(i):
            acc = psum.tile([P, S], F32, name="acc%d" % i)
            for e in range(2):
                c0 = P * (i % 2)
                nc.tensor.matmul_mx(
                    out=acc[:],
                    lhsT=d_codes[i // 2][e][:, c0:c0 + P].bitcast(FP8X4),
                    lhsT_scale=d_planes[i // 2][:, HALF * e + c0:HALF * e + c0 + P],
                    rhs=z_codes[:].bitcast(FP8X4),
                    rhs_scale=z_plane[:],
                    start=(e == 0),
                    stop=(e == 1),
                )
            h = keep.tile([P, S], F32, name="h%d" % i)
            if i == 0:
                nc.scalar.activation(h[:], acc[:], COPY, scale=0.0625)
            else:
                nc.vector.tensor_scalar(h[:], acc[:], 0.0625, None, ALU.mult)
            b = keep.tile([P, W], F32, name="pb%d" % i)
            a = keep.tile([P, W], F32, name="pa%d" % i)
            nc.scalar.activation(b[:], h[:].indirect(n2_t[:]), COPY)
            nc.scalar.activation(a[:], h[:].indirect(n1_t[:]), COPY)
            pa.append(a)
            pb.append(b)

        def finish(i):
            a, b = pa[i], pb[i]
            flip = keep.tile([P, W], F32, name="flip%d" % i)
            den = keep.tile([P, W], F32, name="den%d" % i)
            inv = keep.tile([P, W], F32, name="inv%d" % i)
            ra = keep.tile([P, W], F32, name="ra%d" % i)
            rb = keep.tile([P, W], F32, name="rb%d" % i)
            res = keep.tile([P, S], F32, name="res%d" % i)
            nc.vector.tensor_scalar(flip[:], b[:], -1.0, 0.5, ALU.mult, ALU.add)
            nc.vector.tensor_tensor(rb[:], a[:], b[:], ALU.max)
            nc.vector.scalar_tensor_tensor(den[:], b[:], 0.5, flip[:], ALU.add, ALU.max)
            nc.vector.reciprocal(inv[:], den[:])
            nc.vector.tensor_tensor(ra[:], a[:], inv[:], ALU.mult)
            nc.scalar.activation(res[:].indirect(n2_t[:]), rb[:], COPY)
            nc.scalar.activation(res[:].indirect(n1_t[:]), ra[:], COPY)
            nc.sync.dma_start(out[P * i:P * i + P, :], res[:])

        for i in range(4):
            fetch(i)
        for i in range(4):
            finish(i)
